import numpy as np
import ml_dtypes


def mxq(x, axis, fmt="e4m3"):
    dtype, down = {"e4m3": (ml_dtypes.float8_e4m3fn, 7), "e5m2": (ml_dtypes.float8_e5m2, 14)}[fmt]
    v = np.moveaxis(np.asarray(x, np.float32).astype(ml_dtypes.bfloat16).astype(np.float64), axis, -1)
    blocks = v.reshape(v.shape[:-1] + (-1, 32))
    amax = np.abs(blocks).max(-1, keepdims=True)
    byte = np.maximum(np.where(amax > 0, np.frexp(amax)[1] - 1 + 127, 0) - down, 1)
    scale = np.exp2(byte - 127.0)
    codes = (blocks / scale).astype(np.float32).astype(dtype).astype(np.float64)
    return np.moveaxis((codes * scale).reshape(v.shape), -1, axis)


WIDE = False


def mx_kscale(k):
    if not WIDE:
        return np.ones(k)
    levels = np.array([10, -10, 5, -5, 0])
    if k % 512:
        return np.exp2(np.random.permutation(np.resize(levels, k // 32))).repeat(32)
    a = np.empty((k // 512, 16))
    for p in range(k // 512):
        a[p, :8] = np.random.permutation(np.resize(levels, 8))
        for g in range(8):
            far = levels[np.abs(levels - a[p, g]) >= 10]
            a[p, g + 8] = far[np.random.randint(len(far))]
    return np.exp2(a.ravel()).repeat(32)


def f64(x):
    return np.asarray(x).astype(np.float64)


def striped(idx):
    return np.tile(idx.reshape(-1, 16).T, (8, 1)).astype(np.uint16)


def unstriped(offs):
    return offs[:16].T.reshape(-1).astype(np.int64)


E2M1 = np.array([0.0, 0.5, 1.0, 1.5, 2.0, 3.0, 4.0, 6.0, -0.0, -0.5, -1.0, -1.5, -2.0, -3.0, -4.0, -6.0])


def pack_weight(w, fmt):
    k, n = w.shape
    w = f64(np.asarray(w, np.float32).astype(ml_dtypes.bfloat16)).reshape(k // 32, 32, n)
    amax = np.abs(w).max(1)
    if fmt == "e4m3":
        byte = np.frexp(amax)[1] - 1 + 127 - 7
    else:
        mant, ex = np.frexp(amax / 6.0)
        byte = np.where(mant > 0.5, ex, ex - 1) + 127
    byte = np.clip(np.where(amax > 0, byte, 1), 1, 254)
    scaled = (w * np.exp2(127.0 - byte)[:, None, :]).reshape(k, n).astype(np.float32)
    by_word = np.ascontiguousarray(scaled.reshape(k // 512, 128, 4, n).transpose(0, 1, 3, 2))
    if fmt == "e4m3":
        words = by_word.astype(ml_dtypes.float8_e4m3fn).view(np.uint8)
    else:
        c = by_word.astype(ml_dtypes.float4_e2m1fn).view(np.uint8) & 0xF
        words = (c[..., 0::2] | (c[..., 1::2] << 4)).reshape(k // 512, 128, 2 * n)
    return np.ascontiguousarray(words), np.ascontiguousarray(byte.astype(np.uint8).reshape(k // 512, 16, n))


def unpack_weight(words, scales, fmt):
    g, _, n = scales.shape
    words = np.ascontiguousarray(words).reshape(g, 128, n, -1)
    if fmt == "e4m3":
        vals = words.view(ml_dtypes.float8_e4m3fn).astype(np.float64)
    else:
        nib = np.empty((g, 128, n, 4), np.uint8)
        nib[..., 0::2] = words & 0xF
        nib[..., 1::2] = words >> 4
        vals = E2M1[nib]
    vals = vals * np.repeat(np.exp2(scales.astype(np.float64) - 127.0), 8, axis=1)[..., None]
    return vals.transpose(0, 1, 3, 2).reshape(g * 512, n)


def gelu(v):
    return 0.5 * v * (1.0 + np.tanh(np.sqrt(2.0 / np.pi) * (v + 0.044715 * v**3)))


def bf(x):
    return np.asarray(x, np.float32).astype(ml_dtypes.bfloat16)


def planes(Y):
    n, m = Y.shape
    b = f64(bf(Y)).reshape(n // 32, 32, m)
    amax = np.abs(b).max(1)
    byte = np.clip(np.where(amax > 0, np.frexp(amax)[1] - 1 + 127 - 7, 1), 1, 254)
    codes = (b * np.exp2(127.0 - byte)[:, None, :]).reshape(n, m).astype(np.float32).astype(ml_dtypes.float8_e4m3fn).view(np.uint8)
    words = codes.reshape(n // 512, 128, 4, m).transpose(0, 1, 3, 2)
    return np.ascontiguousarray(words), np.ascontiguousarray(byte.astype(np.uint8).reshape(n // 512, 16, m))


K, K2, T, T3, S, T2, H, N, P = 1024, 512, 2048, 1024, 512, 2048, 1024, 512, 1024

def setup_inputs():
    n = np.random.standard_normal
    s, s2, u = mx_kscale(K)[:, None], mx_kscale(K2)[:, None], mx_kscale(H)[:, None]
    perm = np.random.permutation(T2)
    d = {}
    d["tab_words"], d["tab_scales"] = pack_weight(n((K, T)) * s, "e4m3")
    d["tab2_words"], d["tab2_scales"] = pack_weight(n((K2, T3)) * s2, "e4m3")
    d["offs"] = striped(np.random.permutation(T)[:S])
    d["offs2"] = striped(np.random.permutation(T3)[:S])
    d["offs3"] = striped(perm[:S])
    d["offs4"] = striped(perm[S:2 * S])
    d["offs5"] = striped(np.random.permutation(T2)[:P])
    d["w1"] = (1.5 * n((K, H)) / K**0.5 / s * u.T).astype(np.float32)
    d["w2_words"], d["w2_scales"] = pack_weight(2.0 * n((K2, H)) / K2**0.5 / s2, "e4m3")
    d["gain"] = (1.4 * np.exp(0.5 * n(H)) * u[:, 0]).astype(np.float32)
    d["wg1"] = np.exp(0.3 * n((128, S))).astype(np.float32)
    d["wg2"] = np.exp(0.3 * n((128, S))).astype(np.float32)
    d["page0"] = (n((H, T2)) * u).astype(np.float32)
    d["lean"] = (0.8 * n(H) * u[:, 0]).astype(np.float32)
    d["wa_words"], d["wa_scales"] = pack_weight(0.6 * n((H, N)) / H**0.5 / u * np.exp(0.8 * n(N)), "e2m1")
    d["wb"] = (0.5 * n((H, N)) / H**0.5 / u).astype(np.float32)
    return d

def reference(tab_words, tab_scales, tab2_words, tab2_scales, offs, offs2, offs3, offs4, offs5, w1, w2_words, w2_scales, gain, wg1, wg2, page0, lean, wa_words, wa_scales, wb):
    v = unpack_weight(tab_words, tab_scales, "e4m3")[:, unstriped(offs)]
    v2 = unpack_weight(tab2_words, tab2_scales, "e4m3")[:, unstriped(offs2)]
    h1 = np.abs(mxq(f64(w1), 0, "e4m3").T @ v)
    h2 = f64(gain)[:, None] * np.tanh(unpack_weight(w2_words, w2_scales, "e4m3").T @ v2)
    page = f64(page0).copy()
    page[:, unstriped(offs3)] = np.tile(f64(wg1), (H // 128, 1)) * h1
    page[:, unstriped(offs4)] = np.tile(f64(wg2), (H // 128, 1)) * h2
    x = page[:, unstriped(offs5)] + f64(lean)[:, None]
    xq = mxq(x, 0, "e4m3")
    ya = unpack_weight(wa_words, wa_scales, "e2m1").T @ xq
    yb = mxq(f64(wb), 0, "e4m3").T @ xq
    y = ya * yb + ya + yb
    words, scales = planes(y)
    return y, words, scales

@@ -1,0 +1,303 @@
+from contextlib import ExitStack
+
+import concourse.mybir as mybir
+
+K, K2, T, T3, S, T2, H, N, M = 1024, 512, 2048, 1024, 512, 2048, 1024, 512, 1024
+FLOPS = 2 * (K * H * S + K2 * H * S + 2 * H * N * M)
+
+F32 = mybir.dt.float32
+BF16 = mybir.dt.bfloat16
+I32 = mybir.dt.int32
+U32 = mybir.dt.uint32
+U16 = mybir.dt.uint16
+U8 = mybir.dt.uint8
+FP8X4 = mybir.dt.float8_e4m3fn_x4
+FP4X4 = mybir.dt.float4_e2m1fn_x4
+ACT = mybir.ActivationFunctionType
+MULT = mybir.AluOpType.mult
+ADD = mybir.AluOpType.add
+
+P = 128
+PACK = 4
+KP = P * PACK
+XC = 256
+YC = 128
+ALIGN = 64
+
+
+def tile_list_placement_office_slots_kernel(
+    tc, tab_words, tab_scales, tab2_words, tab2_scales, offs, offs2, offs3, offs4, offs5,
+    w1, w2_words, w2_scales, gain, wg1, wg2, page0, lean, wa_words, wa_scales, wb,
+    out_0, out_1, out_2,
+):
+    nc = tc.nc
+    with ExitStack() as ctx:
+        keep = ctx.enter_context(tc.tile_pool(name="keep", bufs=1))
+        ring = ctx.enter_context(tc.tile_pool(name="ring", bufs=2))
+        psum = ctx.enter_context(tc.psum_pool(name="psum", bufs=8))
+
+        def held(name, shape, dtype):
+            return keep.tile(shape, dtype, name=name, align_bytes=ALIGN)
+
+        def turned(tag, name, shape, dtype, bufs):
+            return ring.tile(shape, dtype, name=name, tag=tag, bufs=bufs, align_bytes=ALIGN)
+
+        def load_list(name, src):
+            tile = held(name, [P, src.shape[1]], U16)
+            nc.sync.dma_start(tile[:], src)
+            return tile
+
+        def words_of(src):
+            return src.rearrange("p c i -> p (c i)").bitcast(I32)
+
+        tab2s = held("tab2s", [P, T3], U8)
+        nc.gpsimd.memset(tab2s[:].bitcast(I32), 0)
+        w2s_raw = held("w2s_raw", [P, KP], U8)
+        nc.gpsimd.memset(w2s_raw[:].bitcast(I32), 0)
+        was_raw = held("was_raw", [P, 2, N], U8)
+        nc.vector.memset(was_raw[:].bitcast(I32), 0)
+        tabs = held("tabs", [P, T], U8)
+        nc.vector.memset(tabs[:].bitcast(I32), 0)
+
+        l2 = load_list("l2", offs2)
+        tab2w = held("tab2w", [P, T3], I32)
+        nc.sync.dma_start(tab2w[:], words_of(tab2_words[0]))
+        for q in range(4):
+            nc.sync.dma_start(tab2s[32 * q : 32 * q + 4, :].bitcast(I32), tab2_scales[0, 4 * q : 4 * q + 4, :].bitcast(I32))
+        w2w_raw = turned("g", "w2w_raw", [P, H], I32, 2)
+        nc.sync.dma_start(w2w_raw[:], words_of(w2_words[0]))
+        for q in range(4):
+            nc.sync.dma_start(
+                w2s_raw[32 * q : 32 * q + 8, :].bitcast(I32),
+                w2_scales[0, 4 * q : 4 * q + 4, :].rearrange("r (b c) -> b r c", b=2).bitcast(I32),
+            )
+        gain_t = held("gain_t", [P, 2, PACK], F32)
+        nc.sync.dma_start(gain_t[:], gain.rearrange("(b p t) -> p b t", b=2, t=PACK))
+
+        def load_dealt(name, src):
+            tile = held(name, [P, PACK, S], F32)
+            for q in range(4):
+                nc.sync.dma_start(tile[32 * q : 32 * (q + 1)], src.rearrange("(q t) j -> q t j", t=PACK))
+            return tile
+
+        page_rows = page0.rearrange("(b p t) c -> b t p c", b=2, t=PACK)
+        pages = {}
+
+        def load_page(s):
+            pages[s] = held("page%d" % s, [P, T2], F32)
+            nc.sync.dma_start(pages[s][:], page_rows[s // PACK, s % PACK])
+
+        load_page(0)
+        l4 = load_list("l4", offs4)
+        wg2d = load_dealt("wg2d", wg2)
+        waw_raw = turned("h", "waw_raw", [P, 2, 2 * N], U8, 4)
+        nc.sync.dma_start(waw_raw[:].bitcast(I32), wa_words.rearrange("a p c -> p a c").bitcast(I32))
+        for q in range(4):
+            nc.sync.dma_start(
+                was_raw[32 * q : 32 * q + 4].bitcast(I32),
+                wa_scales[:, 4 * q : 4 * q + 4, :].rearrange("a r c -> r a c").bitcast(I32),
+            )
+        lean_t = held("lean_t", [P, 2, PACK], F32)
+        nc.sync.dma_start(lean_t[:], lean.rearrange("(b p t) -> p b t", b=2, t=PACK))
+        load_page(1)
+        l1 = load_list("l1", offs)
+        for q in range(4):
+            nc.sync.dma_start(tabs[32 * q : 32 * q + 8, :].bitcast(I32), tab_scales[:, 4 * q : 4 * q + 4, :].bitcast(I32))
+        load_page(2)
+        tabw = []
+        for a in range(2):
+            tabw.append(held("tabw%d" % a, [P, T], I32))
+            nc.sync.dma_start(tabw[a][:], words_of(tab_words[a]))
+        load_page(3)
+
+        raws = {}
+
+        def load_weight(name, src):
+            raws[name] = turned("wraw", name + "_raw", [P, PACK, KP], F32, 3)
+            nc.sync.dma_start(raws[name][:], src.rearrange("(p j) c -> p j c", j=PACK))
+
+        load_weight("w1_00", w1[0:KP, 0:KP])
+        load_weight("w1_10", w1[KP:K, 0:KP])
+        load_page(4)
+        l3 = load_list("l3", offs3)
+        wg1d = load_dealt("wg1d", wg1)
+        l5 = load_list("l5", offs5)
+
+        v2w = held("v2w", [P, S], U32)
+        nc.vector.tensor_copy(v2w[:], tab2w[:].bitcast(U32).indirect(l2[:]))
+        v2s = held("v2s", [P, S], U8)
+        nc.vector.tensor_copy(v2s[:], tab2s[:].indirect(l2[:]))
+        w2w = held("w2w", [P, H], I32)
+        nc.vector.tensor_copy(
+            w2w[:].rearrange("p (b t q) -> p b q t", b=2, t=PACK), w2w_raw[:].rearrange("p (b q t) -> p b q t", b=2, t=PACK)
+        )
+        w2s = held("w2s", [P, KP], U8)
+        nc.vector.tensor_copy(w2s[:].rearrange("p (t q) -> p q t", t=PACK), w2s_raw[:].rearrange("p (q t) -> p q t", t=PACK))
+        waw = held("waw", [P, 2, 2 * N], U8)
+        nc.vector.tensor_copy(
+            waw[:].bitcast(U16).rearrange("p a (t q) -> p a q t", t=PACK), waw_raw[:].bitcast(U16).rearrange("p a (q t) -> p a q t", t=PACK)
+        )
+        was = held("was", [P, 2, N], U8)
+        nc.vector.tensor_copy(
+            was[:].rearrange("p a (t q) -> p a q t", t=PACK), was_raw[:].rearrange("p a (q t) -> p a q t", t=PACK)
+        )
+
+        def place_h2(s):
+            cols = slice(s * P, (s + 1) * P)
+            bank = psum.tile([P, S], F32, name="h2ps%d" % s, tag="bank")
+            nc.tensor.matmul_mx(
+                out=bank[:], lhsT=w2w[:, cols].bitcast(FP8X4), lhsT_scale=w2s[4 * (s // PACK) : P, (s % PACK) * P : (s % PACK + 1) * P],
+                rhs=v2w[:].bitcast(FP8X4), rhs_scale=v2s[:], start=True, stop=True,
+            )
+            h2 = turned("h", "h2_%d" % s, [P, S], F32, 4)
+            nc.scalar.activation(h2[:], bank[:], ACT.Tanh)
+            nc.scalar.activation(h2[:], h2[:], ACT.Copy, scale=gain_t[:, s // PACK, s % PACK : s % PACK + 1])
+            nc.vector.tensor_tensor(pages[s][:].indirect(l4[:]), h2[:], wg2d[:, s % PACK, :], MULT)
+
+        codes = {}
+        grouped = {}
+
+        def round_weight(name):
+            grouped[name] = turned("wgrp", name + "_grp", [P, PACK * KP], BF16, 2)
+            nc.scalar.copy(
+                grouped[name][:].rearrange("p (t m j) -> p m t j", t=PACK, j=PACK),
+                raws[name][:].rearrange("p j (m t) -> p m t j", t=PACK),
+            )
+
+        def quantise_weight(name):
+            words = held(name + "_w", [P, KP], U32)
+            scales = held(name + "_s", [P, KP], U8)
+            nc.vector.quantize_mx(out=words[:].bitcast(FP8X4), scales=scales[:], in_=grouped[name][:])
+            codes[name] = (words, scales)
+
+        for s in range(3):
+            place_h2(s)
+        vw = []
+        for a in range(2):
+            vw.append(held("vw%d" % a, [P, S], U32))
+            nc.vector.tensor_copy(vw[a][:], tabw[a][:].bitcast(U32).indirect(l1[:]))
+        vs = held("vs", [P, S], U8)
+        nc.vector.tensor_copy(vs[:], tabs[:].indirect(l1[:]))
+        place_h2(3)
+        round_weight("w1_00")
+        quantise_weight("w1_00")
+        load_weight("w1_01", w1[0:KP, KP:H])
+        round_weight("w1_10")
+        quantise_weight("w1_10")
+        load_weight("w1_11", w1[KP:K, KP:H])
+        place_h2(4)
+
+        def place_h1(s):
+            b, t = divmod(s, PACK)
+            cols = slice(t * P, (t + 1) * P)
+            bank = psum.tile([P, S], F32, name="h1ps%d" % s, tag="bank")
+            for a in range(2):
+                words, scales = codes["w1_%d%d" % (a, b)]
+                nc.tensor.matmul_mx(
+                    out=bank[:], lhsT=words[:, cols].bitcast(FP8X4), lhsT_scale=scales[:, cols],
+                    rhs=vw[a][:].bitcast(FP8X4), rhs_scale=vs[4 * a : P, :], start=(a == 0), stop=(a == 1),
+                )
+            h1 = turned("h", "h1_%d" % s, [P, S], F32, 4)
+            nc.scalar.activation(h1[:], bank[:], ACT.Abs)
+            nc.vector.tensor_tensor(pages[s][:].indirect(l3[:]), h1[:], wg1d[:, t, :], MULT)
+
+        xi0 = held("xi0", [P, M, PACK], BF16)
+        xi1 = [held("xi1_%d" % c, [P, XC, PACK], BF16) for c in range(M // XC)]
+
+        def shift(dst, src, s):
+            b, t = divmod(s, PACK)
+            nc.scalar.activation(dst[:, :, t], src, ACT.Identity, bias=lean_t[:, b, t : t + 1])
+
+        def read_page(s):
+            g = turned("g", "g%d" % s, [P, M], F32, 2)
+            nc.vector.tensor_copy(g[:], pages[s][:].indirect(l5[:]))
+            if s < PACK:
+                shift(xi0, g[:], s)
+            else:
+                for c in range(M // XC):
+                    shift(xi1[c], g[:, c * XC : (c + 1) * XC], s)
+
+        place_h1(0)
+        read_page(0)
+        round_weight("w1_01")
+        quantise_weight("w1_01")
+        load_weight("wb_0", wb[0:KP, :])
+        place_h1(1)
+        read_page(1)
+        round_weight("w1_11")
+        quantise_weight("w1_11")
+        load_weight("wb_1", wb[KP:H, :])
+        for s in range(5, 8):
+            load_page(s)
+        place_h1(2)
+        read_page(2)
+        round_weight("wb_0")
+        quantise_weight("wb_0")
+        place_h1(3)
+        read_page(3)
+        round_weight("wb_1")
+        quantise_weight("wb_1")
+        place_h1(4)
+        xq0 = held("xq0", [P, M], U32)
+        xs0 = held("xs0", [P, M], U8)
+        nc.vector.quantize_mx(out=xq0[:].bitcast(FP8X4), scales=xs0[:], in_=xi0[:].rearrange("p m t -> p (m t)"))
+        read_page(4)
+        for s in range(5, 7):
+            place_h2(s)
+            place_h1(s)
+            read_page(s)
+        place_h2(7)
+        place_h1(7)
+
+        xq1 = []
+        for c in range(M // XC):
+            g = held("glast%d" % c, [P, XC], F32)
+            nc.vector.tensor_copy(g[:], pages[7][:].indirect(l5[:, c * XC // 16 : (c + 1) * XC // 16]))
+            shift(xi1[c], g[:], 7)
+            words = held("xq1_%d" % c, [P, XC], U32)
+            scales = held("xs1_%d" % c, [P, XC], U8)
+            nc.vector.quantize_mx(out=words[:].bitcast(FP8X4), scales=scales[:], in_=xi1[c][:].rearrange("p m t -> p (m t)"))
+            xq1.append((words, scales))
+
+        yq = held("yq", [P, M], U32)
+        ys = held("ys", [P, M], U8)
+        y_rows = out_0.rearrange("(p t) m -> p t m", t=PACK)
+        y_words = words_of(out_1[0])
+        for c in range(M // YC):
+            cols = slice(c * YC, (c + 1) * YC)
+            ya = psum.tile([P, PACK, YC], F32, name="ya%d" % c, tag="bank")
+            yb = psum.tile([P, PACK, YC], F32, name="yb%d" % c, tag="bank")
+            for a in range(2):
+                if a == 0:
+                    x_words, x_scales = xq0[:, cols], xs0[:, cols]
+                else:
+                    part = slice(c * YC % XC, c * YC % XC + YC)
+                    x_words, x_scales = xq1[c * YC // XC][0][:, part], xq1[c * YC // XC][1][:, part]
+                b_words, b_scales = codes["wb_%d" % a]
+                for t in range(PACK):
+                    nc.tensor.matmul_mx(
+                        out=yb[:, t, :], lhsT=b_words[:, t * P : (t + 1) * P].bitcast(FP8X4), lhsT_scale=b_scales[:, t * P : (t + 1) * P],
+                        rhs=x_words.bitcast(FP8X4), rhs_scale=x_scales, start=(a == 0 and t == 0), stop=(a == 1 and t == PACK - 1),
+                    )
+                for t in range(PACK):
+                    nc.tensor.matmul_mx(
+                        out=ya[:, t, :], lhsT=waw[:, a, 2 * t * P : 2 * (t + 1) * P].bitcast(FP4X4), lhsT_scale=was[:, a, t * P : (t + 1) * P],
+                        rhs=x_words.bitcast(FP8X4), rhs_scale=x_scales, start=(a == 0 and t == 0), stop=(a == 1 and t == PACK - 1),
+                    )
+            yb_sb = turned("h", "yb_sb%d" % c, [P, PACK, YC], F32, 4)
+            nc.scalar.copy(yb_sb[:], yb[:])
+            u = turned("u", "u%d" % c, [P, PACK, YC], F32, 2)
+            nc.vector.scalar_tensor_tensor(u[:], yb_sb[:], 1.0, ya[:], ADD, MULT)
+            y = turned("y", "y%d" % c, [P, PACK, YC], F32, 4)
+            nc.vector.tensor_tensor(y[:], u[:], yb_sb[:], ADD)
+            nc.sync.dma_start(y_rows[:, :, cols], y[:])
+            yi = turned("yi", "yi%d" % c, [P, YC, PACK], BF16, 3)
+            nc.scalar.copy(
+                yi[:].rearrange("p (c i) t -> p c t i", i=4), y[:].rearrange("p t (c i) -> p c t i", i=4)
+            )
+            nc.vector.quantize_mx(out=yq[:, cols].bitcast(FP8X4), scales=ys[:, cols], in_=yi[:].rearrange("p m t -> p (m t)"))
+            if c % 2 == 1:
+                pair = slice((c - 1) * YC, (c + 1) * YC)
+                nc.sync.dma_start(y_words[:, pair], yq[:, pair].bitcast(I32))
+        for q in range(4):
+            nc.scalar.dma_start(out_2[0, 4 * q : 4 * q + 4, :].bitcast(I32), ys[32 * q : 32 * q + 4, :].bitcast(I32))

@@ -52,9 +52,9 @@ def tile_list_placement_office_slots_kernel(
 
         tab2s = held("tab2s", [P, T3], U8)
         nc.gpsimd.memset(tab2s[:].bitcast(I32), 0)
-        w2s_raw = held("w2s_raw", [P, KP], U8)
+        w2s_raw = turned("yi", "w2s_raw", [P, KP], U8, 3)
         nc.gpsimd.memset(w2s_raw[:].bitcast(I32), 0)
-        was_raw = held("was_raw", [P, 2, N], U8)
+        was_raw = turned("yi", "was_raw", [P, 2, N], U8, 3)
         nc.vector.memset(was_raw[:].bitcast(I32), 0)
         tabs = held("tabs", [P, T], U8)
         nc.vector.memset(tabs[:].bitcast(I32), 0)
@@ -64,7 +64,7 @@ def tile_list_placement_office_slots_kernel(
         nc.sync.dma_start(tab2w[:], words_of(tab2_words[0]))
         for q in range(4):
             nc.sync.dma_start(tab2s[32 * q : 32 * q + 4, :].bitcast(I32), tab2_scales[0, 4 * q : 4 * q + 4, :].bitcast(I32))
-        w2w_raw = turned("g", "w2w_raw", [P, H], I32, 2)
+        w2w_raw = turned("stage_c", "w2w_raw", [P, H], I32, 1)
         nc.sync.dma_start(w2w_raw[:], words_of(w2_words[0]))
         for q in range(4):
             nc.sync.dma_start(
@@ -74,11 +74,11 @@ def tile_list_placement_office_slots_kernel(
         gain_t = held("gain_t", [P, 2, PACK], F32)
         nc.sync.dma_start(gain_t[:], gain.rearrange("(b p t) -> p b t", b=2, t=PACK))
 
-        def load_dealt(name, src):
-            tile = held(name, [P, PACK, S], F32)
+        def load_dealt(name, src, first, last):
+            tile = held(name, [P, last - first, S], F32)
             for q in range(4):
-                nc.sync.dma_start(tile[32 * q : 32 * (q + 1)], src.rearrange("(q t) j -> q t j", t=PACK))
-            return tile
+                nc.sync.dma_start(tile[32 * q : 32 * (q + 1)], src.rearrange("(q t) j -> q t j", t=PACK)[:, first:last, :])
+            return [tile[:, t, :] for t in range(last - first)]
 
         page_rows = page0.rearrange("(b p t) c -> b t p c", b=2, t=PACK)
         pages = {}
@@ -87,41 +87,44 @@ def tile_list_placement_office_slots_kernel(
             pages[s] = held("page%d" % s, [P, T2], F32)
             nc.sync.dma_start(pages[s][:], page_rows[s // PACK, s % PACK])
 
-        load_page(0)
-        l4 = load_list("l4", offs4)
-        wg2d = load_dealt("wg2d", wg2)
-        waw_raw = turned("h", "waw_raw", [P, 2, 2 * N], U8, 4)
-        nc.sync.dma_start(waw_raw[:].bitcast(I32), wa_words.rearrange("a p c -> p a c").bitcast(I32))
-        for q in range(4):
-            nc.sync.dma_start(
-                was_raw[32 * q : 32 * q + 4].bitcast(I32),
-                wa_scales[:, 4 * q : 4 * q + 4, :].rearrange("a r c -> r a c").bitcast(I32),
-            )
-        lean_t = held("lean_t", [P, 2, PACK], F32)
-        nc.sync.dma_start(lean_t[:], lean.rearrange("(b p t) -> p b t", b=2, t=PACK))
-        load_page(1)
-        l1 = load_list("l1", offs)
-        for q in range(4):
-            nc.sync.dma_start(tabs[32 * q : 32 * q + 8, :].bitcast(I32), tab_scales[:, 4 * q : 4 * q + 4, :].bitcast(I32))
-        load_page(2)
-        tabw = []
-        for a in range(2):
-            tabw.append(held("tabw%d" % a, [P, T], I32))
-            nc.sync.dma_start(tabw[a][:], words_of(tab_words[a]))
-        load_page(3)
-
         raws = {}
 
         def load_weight(name, src):
             raws[name] = turned("wraw", name + "_raw", [P, PACK, KP], F32, 3)
             nc.sync.dma_start(raws[name][:], src.rearrange("(p j) c -> p j c", j=PACK))
 
+        load_page(0)
+        l4 = load_list("l4", offs4)
+        wg2d = load_dealt("wg2_first", wg2, 0, 1)
+        load_page(4)
+        wg2d = wg2d + load_dealt("wg2_rest", wg2, 1, PACK)
+        load_page(1)
+        l1 = load_list("l1", offs)
+        tabw = []
+        for a in range(2):
+            tabw.append(held("tabw%d" % a, [P, T], I32))
+            nc.sync.dma_start(tabw[a][:], words_of(tab_words[a]))
+            for q in range(2 * a, 2 * a + 2):
+                nc.sync.dma_start(tabs[32 * q : 32 * q + 8, :].bitcast(I32), tab_scales[:, 4 * q : 4 * q + 4, :].bitcast(I32))
+        load_page(2)
         load_weight("w1_00", w1[0:KP, 0:KP])
         load_weight("w1_10", w1[KP:K, 0:KP])
-        load_page(4)
+        load_page(3)
+        load_page(5)
         l3 = load_list("l3", offs3)
-        wg1d = load_dealt("wg1d", wg1)
+        wg1d = load_dealt("wg1_first", wg1, 0, 1)
         l5 = load_list("l5", offs5)
+        wg1d = wg1d + load_dealt("wg1_rest", wg1, 1, PACK)
+        lean_t = held("lean_t", [P, 2, PACK], F32)
+        nc.sync.dma_start(lean_t[:], lean.rearrange("(b p t) -> p b t", b=2, t=PACK))
+        load_weight("w1_01", w1[0:KP, KP:H])
+        waw_raw = turned("y", "waw_raw", [P, 2, 2 * N], U8, 4)
+        nc.sync.dma_start(waw_raw[:].bitcast(I32), wa_words.rearrange("a p c -> p a c").bitcast(I32))
+        for q in range(4):
+            nc.sync.dma_start(
+                was_raw[32 * q : 32 * q + 4].bitcast(I32),
+                wa_scales[:, 4 * q : 4 * q + 4, :].rearrange("a r c -> r a c").bitcast(I32),
+            )
 
         v2w = held("v2w", [P, S], U32)
         nc.vector.tensor_copy(v2w[:], tab2w[:].bitcast(U32).indirect(l2[:]))
@@ -129,65 +132,74 @@ def tile_list_placement_office_slots_kernel(
         nc.vector.tensor_copy(v2s[:], tab2s[:].indirect(l2[:]))
         w2w = held("w2w", [P, H], I32)
         nc.vector.tensor_copy(
-            w2w[:].rearrange("p (b t q) -> p b q t", b=2, t=PACK), w2w_raw[:].rearrange("p (b q t) -> p b q t", b=2, t=PACK)
+            w2w[:].rearrange("p (b t q i) -> p b q t i", b=2, t=PACK, i=4), w2w_raw[:].rearrange("p (b q i t) -> p b q t i", b=2, t=PACK, i=4)
         )
         w2s = held("w2s", [P, KP], U8)
-        nc.vector.tensor_copy(w2s[:].rearrange("p (t q) -> p q t", t=PACK), w2s_raw[:].rearrange("p (q t) -> p q t", t=PACK))
+        nc.vector.tensor_copy(
+            w2s[:].rearrange("p (t q i) -> p q t i", t=PACK, i=16), w2s_raw[:].rearrange("p (q i t) -> p q t i", t=PACK, i=16)
+        )
         waw = held("waw", [P, 2, 2 * N], U8)
-        nc.vector.tensor_copy(
-            waw[:].bitcast(U16).rearrange("p a (t q) -> p a q t", t=PACK), waw_raw[:].bitcast(U16).rearrange("p a (q t) -> p a q t", t=PACK)
-        )
         was = held("was", [P, 2, N], U8)
-        nc.vector.tensor_copy(
-            was[:].rearrange("p a (t q) -> p a q t", t=PACK), was_raw[:].rearrange("p a (q t) -> p a q t", t=PACK)
-        )
 
-        def place_h2(s):
-            cols = slice(s * P, (s + 1) * P)
-            bank = psum.tile([P, S], F32, name="h2ps%d" % s, tag="bank")
-            nc.tensor.matmul_mx(
-                out=bank[:], lhsT=w2w[:, cols].bitcast(FP8X4), lhsT_scale=w2s[4 * (s // PACK) : P, (s % PACK) * P : (s % PACK + 1) * P],
-                rhs=v2w[:].bitcast(FP8X4), rhs_scale=v2s[:], start=True, stop=True,
+        def deal_wa():
+            nc.vector.tensor_copy(
+                waw[:].bitcast(U16).rearrange("p a (t q i) -> p a q t i", t=PACK, i=8),
+                waw_raw[:].bitcast(U16).rearrange("p a (q i t) -> p a q t i", t=PACK, i=8),
             )
-            h2 = turned("h", "h2_%d" % s, [P, S], F32, 4)
-            nc.scalar.activation(h2[:], bank[:], ACT.Tanh)
-            nc.scalar.activation(h2[:], h2[:], ACT.Copy, scale=gain_t[:, s // PACK, s % PACK : s % PACK + 1])
-            nc.vector.tensor_tensor(pages[s][:].indirect(l4[:]), h2[:], wg2d[:, s % PACK, :], MULT)
+            nc.vector.tensor_copy(
+                was[:].rearrange("p a (t q i) -> p a q t i", t=PACK, i=16), was_raw[:].rearrange("p a (q i t) -> p a q t i", t=PACK, i=16)
+            )
+
+        def place_h2(s, first=0, last=S, h2=None):
+            b, t = divmod(s, PACK)
+            name = "%d_%d" % (s, first)
+            bank = psum.tile([P, last - first], F32, name="h2ps" + name, tag="bank")
+            nc.tensor.matmul_mx(
+                out=bank[:], lhsT=w2w[:, s * P : (s + 1) * P].bitcast(FP8X4), lhsT_scale=w2s[4 * b : P, t * P : (t + 1) * P],
+                rhs=v2w[:, first:last].bitcast(FP8X4), rhs_scale=v2s[:, first:last], start=True, stop=True,
+            )
+            if h2 is None:
+                h2 = turned("h", "h2_" + name, [P, last - first], F32, 5)[:]
+            nc.scalar.activation(h2, bank[:], ACT.Tanh)
+            nc.scalar.activation(h2, h2, ACT.Copy, scale=gain_t[:, b, t : t + 1])
+            nc.vector.tensor_tensor(pages[s][:].indirect(l4[:, first // 16 : last // 16]), h2, wg2d[t][:, first:last], MULT)
 
         codes = {}
         grouped = {}
 
-        def round_weight(name):
-            grouped[name] = turned("wgrp", name + "_grp", [P, PACK * KP], BF16, 2)
+        def round_weight(name, tile=None):
+            grouped[name] = turned("stage_" + "ab"[int(name[3])], name + "_grp", [P, PACK * KP], BF16, 1)[:] if tile is None else tile
             nc.scalar.copy(
-                grouped[name][:].rearrange("p (t m j) -> p m t j", t=PACK, j=PACK),
+                grouped[name].rearrange("p (t m j) -> p m t j", t=PACK, j=PACK),
                 raws[name][:].rearrange("p j (m t) -> p m t j", t=PACK),
             )
 
         def quantise_weight(name):
             words = held(name + "_w", [P, KP], U32)
             scales = held(name + "_s", [P, KP], U8)
-            nc.vector.quantize_mx(out=words[:].bitcast(FP8X4), scales=scales[:], in_=grouped[name][:])
+            nc.vector.quantize_mx(out=words[:].bitcast(FP8X4), scales=scales[:], in_=grouped[name])
             codes[name] = (words, scales)
 
-        for s in range(3):
-            place_h2(s)
+        place_h2(0, 0, S // 2)
+        place_h2(0, S // 2, S)
+        place_h2(4)
+        place_h2(1)
         vw = []
         for a in range(2):
             vw.append(held("vw%d" % a, [P, S], U32))
             nc.vector.tensor_copy(vw[a][:], tabw[a][:].bitcast(U32).indirect(l1[:]))
         vs = held("vs", [P, S], U8)
         nc.vector.tensor_copy(vs[:], tabs[:].indirect(l1[:]))
-        place_h2(3)
+        place_h2(2)
         round_weight("w1_00")
+        place_h2(3)
         quantise_weight("w1_00")
-        load_weight("w1_01", w1[0:KP, KP:H])
         round_weight("w1_10")
         quantise_weight("w1_10")
         load_weight("w1_11", w1[KP:K, KP:H])
-        place_h2(4)
+        place_h2(5)
 
-        def place_h1(s):
+        def place_h1(s, h1=None):
             b, t = divmod(s, PACK)
             cols = slice(t * P, (t + 1) * P)
             bank = psum.tile([P, S], F32, name="h1ps%d" % s, tag="bank")
@@ -197,63 +209,71 @@ def tile_list_placement_office_slots_kernel(
                     out=bank[:], lhsT=words[:, cols].bitcast(FP8X4), lhsT_scale=scales[:, cols],
                     rhs=vw[a][:].bitcast(FP8X4), rhs_scale=vs[4 * a : P, :], start=(a == 0), stop=(a == 1),
                 )
-            h1 = turned("h", "h1_%d" % s, [P, S], F32, 4)
-            nc.scalar.activation(h1[:], bank[:], ACT.Abs)
-            nc.vector.tensor_tensor(pages[s][:].indirect(l3[:]), h1[:], wg1d[:, t, :], MULT)
+            if h1 is None:
+                h1 = turned("h", "h1_%d" % s, [P, S], F32, 5)[:]
+            nc.scalar.activation(h1, bank[:], ACT.Abs)
+            nc.vector.tensor_tensor(pages[s][:].indirect(l3[:]), h1, wg1d[t], MULT)
 
         xi0 = held("xi0", [P, M, PACK], BF16)
+        xp0 = turned("planes", "xp0", [P, PACK, M], BF16, 1)
         xi1 = [held("xi1_%d" % c, [P, XC, PACK], BF16) for c in range(M // XC)]
 
         def shift(dst, src, s):
             b, t = divmod(s, PACK)
-            nc.scalar.activation(dst[:, :, t], src, ACT.Identity, bias=lean_t[:, b, t : t + 1])
+            nc.scalar.activation(dst, src, ACT.Identity, bias=lean_t[:, b, t : t + 1])
 
-        def read_page(s):
-            g = turned("g", "g%d" % s, [P, M], F32, 2)
-            nc.vector.tensor_copy(g[:], pages[s][:].indirect(l5[:]))
+        def read_page(s, g=None):
+            if g is None:
+                g = turned("stage_" + "cababa"[s], "g%d" % s, [P, M], F32, 1)[:]
+            nc.vector.tensor_copy(g, pages[s][:].indirect(l5[:]))
             if s < PACK:
-                shift(xi0, g[:], s)
+                shift(xp0[:, s, :], g, s)
             else:
                 for c in range(M // XC):
-                    shift(xi1[c], g[:, c * XC : (c + 1) * XC], s)
+                    shift(xi1[c][:, :, s % PACK], g[:, c * XC : (c + 1) * XC], s)
 
         place_h1(0)
         read_page(0)
         round_weight("w1_01")
         quantise_weight("w1_01")
-        load_weight("wb_0", wb[0:KP, :])
         place_h1(1)
         read_page(1)
         round_weight("w1_11")
         quantise_weight("w1_11")
+        load_weight("wb_0", wb[0:KP, :])
+        load_page(6)
         load_weight("wb_1", wb[KP:H, :])
-        for s in range(5, 8):
-            load_page(s)
+        load_page(7)
         place_h1(2)
         read_page(2)
-        round_weight("wb_0")
-        quantise_weight("wb_0")
+        deal_wa()
         place_h1(3)
         read_page(3)
-        round_weight("wb_1")
-        quantise_weight("wb_1")
+        nc.scalar.copy(xi0[:].rearrange("p (c i) t -> p c t i", i=4), xp0[:].rearrange("p t (c i) -> p c t i", i=4))
         place_h1(4)
+        read_page(4)
+        place_h1(5)
         xq0 = held("xq0", [P, M], U32)
         xs0 = held("xs0", [P, M], U8)
         nc.vector.quantize_mx(out=xq0[:].bitcast(FP8X4), scales=xs0[:], in_=xi0[:].rearrange("p m t -> p (m t)"))
-        read_page(4)
-        for s in range(5, 7):
-            place_h2(s)
-            place_h1(s)
-            read_page(s)
-        place_h2(7)
-        place_h1(7)
+        wb_grp = turned("planes", "wb_grp", [P, 2 * PACK * KP], BF16, 1)
+        place_h2(6)
+        round_weight("wb_0", wb_grp[:, : PACK * KP])
+        read_page(5)
+        place_h1(6)
+        round_weight("wb_1", wb_grp[:, PACK * KP :])
+        quantise_weight("wb_0")
+        quantise_weight("wb_1")
+        tail = turned("planes", "tail", [P, M + 2 * S], F32, 1)
+        read_page(6, tail[:, :M])
+        place_h1(7, tail[:, M : M + S])
+        place_h2(7, h2=tail[:, M + S :])
 
         xq1 = []
         for c in range(M // XC):
             g = held("glast%d" % c, [P, XC], F32)
             nc.vector.tensor_copy(g[:], pages[7][:].indirect(l5[:, c * XC // 16 : (c + 1) * XC // 16]))
-            shift(xi1[c], g[:], 7)
+            shift(xi1[c][:, :, PACK - 1], g[:], 7)
             words = held("xq1_%d" % c, [P, XC], U32)
             scales = held("xs1_%d" % c, [P, XC], U8)
             nc.vector.quantize_mx(out=words[:].bitcast(FP8X4), scales=scales[:], in_=xi1[c][:].rearrange("p m t -> p (m t)"))
@@ -284,12 +304,11 @@ def tile_list_placement_office_slots_kernel(
                         out=ya[:, t, :], lhsT=waw[:, a, 2 * t * P : 2 * (t + 1) * P].bitcast(FP4X4), lhsT_scale=was[:, a, t * P : (t + 1) * P],
                         rhs=x_words.bitcast(FP8X4), rhs_scale=x_scales, start=(a == 0 and t == 0), stop=(a == 1 and t == PACK - 1),
                     )
-            yb_sb = turned("h", "yb_sb%d" % c, [P, PACK, YC], F32, 4)
+            yb_sb = turned("h", "yb_sb%d" % c, [P, PACK, YC], F32, 5)
             nc.scalar.copy(yb_sb[:], yb[:])
-            u = turned("u", "u%d" % c, [P, PACK, YC], F32, 2)
-            nc.vector.scalar_tensor_tensor(u[:], yb_sb[:], 1.0, ya[:], ADD, MULT)
             y = turned("y", "y%d" % c, [P, PACK, YC], F32, 4)
-            nc.vector.tensor_tensor(y[:], u[:], yb_sb[:], ADD)
+            nc.vector.scalar_tensor_tensor(y[:], yb_sb[:], 1.0, ya[:], ADD, MULT)
+            nc.vector.tensor_tensor(y[:], y[:], yb_sb[:], ADD)
             nc.sync.dma_start(y_rows[:, :, cols], y[:])
             yi = turned("yi", "yi%d" % c, [P, YC, PACK], BF16, 3)
             nc.scalar.copy(

@@ -60,7 +60,7 @@ def tile_list_placement_office_slots_kernel(
         nc.vector.memset(tabs[:].bitcast(I32), 0)
 
         l2 = load_list("l2", offs2)
-        tab2w = held("tab2w", [P, T3], I32)
+        tab2w = turned("tab2w", "tab2w", [P, T3], I32, 1)
         nc.sync.dma_start(tab2w[:], words_of(tab2_words[0]))
         for q in range(4):
             nc.sync.dma_start(tab2s[32 * q : 32 * q + 4, :].bitcast(I32), tab2_scales[0, 4 * q : 4 * q + 4, :].bitcast(I32))
@@ -74,10 +74,11 @@ def tile_list_placement_office_slots_kernel(
         gain_t = held("gain_t", [P, 2, PACK], F32)
         nc.sync.dma_start(gain_t[:], gain.rearrange("(b p t) -> p b t", b=2, t=PACK))
 
-        def load_dealt(name, src, first, last):
-            tile = held(name, [P, last - first, S], F32)
-            for q in range(4):
-                nc.sync.dma_start(tile[32 * q : 32 * (q + 1)], src.rearrange("(q t) j -> q t j", t=PACK)[:, first:last, :])
+        def load_dealt(tag, name, src, first, last, upper_queue):
+            tile = turned(tag, name, [P, last - first, S], F32, 1)
+            for q in (0, 2, 1, 3):
+                queue = nc.sync if q < 2 else upper_queue
+                queue.dma_start(tile[32 * q : 32 * (q + 1)], src.rearrange("(q t) j -> q t j", t=PACK)[:, first:last, :])
             return [tile[:, t, :] for t in range(last - first)]
 
         page_rows = page0.rearrange("(b p t) c -> b t p c", b=2, t=PACK)
@@ -95,39 +96,27 @@ def tile_list_placement_office_slots_kernel(
 
         load_page(0)
         l4 = load_list("l4", offs4)
-        wg2d = load_dealt("wg2_first", wg2, 0, 1)
+        wg2d = load_dealt("wg2_first", "wg2_first", wg2, 0, 1, nc.sync)
         load_page(4)
-        wg2d = wg2d + load_dealt("wg2_rest", wg2, 1, PACK)
+        v2w = held("v2w", [P, S], U32)
+        nc.vector.tensor_copy(v2w[:], tab2w[:].bitcast(U32).indirect(l2[:]))
+        wg2d = wg2d + load_dealt("tab2w", "wg2_rest", wg2, 1, PACK, nc.gpsimd)
         load_page(1)
         l1 = load_list("l1", offs)
         tabw = []
         for a in range(2):
-            tabw.append(held("tabw%d" % a, [P, T], I32))
+            tabw.append(turned("tabw%d" % a, "tabw%d" % a, [P, T], I32, 1))
             nc.sync.dma_start(tabw[a][:], words_of(tab_words[a]))
             for q in range(2 * a, 2 * a + 2):
                 nc.sync.dma_start(tabs[32 * q : 32 * q + 8, :].bitcast(I32), tab_scales[:, 4 * q : 4 * q + 4, :].bitcast(I32))
         load_page(2)
+        load_page(3)
         load_weight("w1_00", w1[0:KP, 0:KP])
         load_weight("w1_10", w1[KP:K, 0:KP])
-        load_page(3)
         load_page(5)
+        load_page(6)
         l3 = load_list("l3", offs3)
-        wg1d = load_dealt("wg1_first", wg1, 0, 1)
-        l5 = load_list("l5", offs5)
-        wg1d = wg1d + load_dealt("wg1_rest", wg1, 1, PACK)
-        lean_t = held("lean_t", [P, 2, PACK], F32)
-        nc.sync.dma_start(lean_t[:], lean.rearrange("(b p t) -> p b t", b=2, t=PACK))
-        load_weight("w1_01", w1[0:KP, KP:H])
-        waw_raw = turned("y", "waw_raw", [P, 2, 2 * N], U8, 4)
-        nc.sync.dma_start(waw_raw[:].bitcast(I32), wa_words.rearrange("a p c -> p a c").bitcast(I32))
-        for q in range(4):
-            nc.sync.dma_start(
-                was_raw[32 * q : 32 * q + 4].bitcast(I32),
-                wa_scales[:, 4 * q : 4 * q + 4, :].rearrange("a r c -> r a c").bitcast(I32),
-            )
 
-        v2w = held("v2w", [P, S], U32)
-        nc.vector.tensor_copy(v2w[:], tab2w[:].bitcast(U32).indirect(l2[:]))
         v2s = held("v2s", [P, S], U8)
         nc.vector.tensor_copy(v2s[:], tab2s[:].indirect(l2[:]))
         w2w = held("w2w", [P, H], I32)
@@ -190,16 +179,34 @@ def tile_list_placement_office_slots_kernel(
             nc.vector.tensor_copy(vw[a][:], tabw[a][:].bitcast(U32).indirect(l1[:]))
         vs = held("vs", [P, S], U8)
         nc.vector.tensor_copy(vs[:], tabs[:].indirect(l1[:]))
+        wg1d = load_dealt("tabw0", "wg1d", wg1, 0, PACK, nc.gpsimd)
+        l5 = load_list("l5", offs5)
+        load_page(7)
+        lean_t = held("lean_t", [P, 2, PACK], F32)
+        nc.sync.dma_start(lean_t[:], lean.rearrange("(b p t) -> p b t", b=2, t=PACK))
+        load_weight("wb_0", wb[0:KP, :])
+        load_weight("wb_1", wb[KP:H, :])
+        load_weight("w1_01", w1[0:KP, KP:H])
+        load_weight("w1_11", w1[KP:K, KP:H])
+        waw_raw = turned("y", "waw_raw", [P, 2, 2 * N], U8, 4)
+        nc.sync.dma_start(waw_raw[:].bitcast(I32), wa_words.rearrange("a p c -> p a c").bitcast(I32))
+        for q in range(4):
+            nc.sync.dma_start(
+                was_raw[32 * q : 32 * q + 4].bitcast(I32),
+                wa_scales[:, 4 * q : 4 * q + 4, :].rearrange("a r c -> r a c").bitcast(I32),
+            )
+
         place_h2(2)
-        round_weight("w1_00")
         place_h2(3)
+        round_weight("w1_00")
         quantise_weight("w1_00")
+        place_h2(5)
         round_weight("w1_10")
         quantise_weight("w1_10")
-        load_weight("w1_11", w1[KP:K, KP:H])
-        place_h2(5)
+        place_h2(6)
+        place_h2(7)
 
-        def place_h1(s, h1=None):
+        def make_h1(s, h1=None):
             b, t = divmod(s, PACK)
             cols = slice(t * P, (t + 1) * P)
             bank = psum.tile([P, S], F32, name="h1ps%d" % s, tag="bank")
@@ -212,10 +219,15 @@ def tile_list_placement_office_slots_kernel(
             if h1 is None:
                 h1 = turned("h", "h1_%d" % s, [P, S], F32, 5)[:]
             nc.scalar.activation(h1, bank[:], ACT.Abs)
-            nc.vector.tensor_tensor(pages[s][:].indirect(l3[:]), h1, wg1d[t], MULT)
+            return h1
 
-        xi0 = held("xi0", [P, M, PACK], BF16)
-        xp0 = turned("planes", "xp0", [P, PACK, M], BF16, 1)
+        def put_h1(s, h1):
+            nc.vector.tensor_tensor(pages[s][:].indirect(l3[:]), h1, wg1d[s % PACK], MULT)
+
+        def place_h1(s):
+            put_h1(s, make_h1(s))
+
+        xp0 = held("xp0", [P, PACK, M], BF16)
         xi1 = [held("xi1_%d" % c, [P, XC, PACK], BF16) for c in range(M // XC)]
 
         def shift(dst, src, s):
@@ -234,40 +246,35 @@ def tile_list_placement_office_slots_kernel(
 
         place_h1(0)
         read_page(0)
+        wb_grp = turned("wide", "wb_grp", [P, 2 * PACK * KP], BF16, 1)
+        round_weight("wb_0", wb_grp[:, : PACK * KP])
+        round_weight("wb_1", wb_grp[:, PACK * KP :])
+        quantise_weight("wb_0")
+        quantise_weight("wb_1")
         round_weight("w1_01")
         quantise_weight("w1_01")
         place_h1(1)
         read_page(1)
         round_weight("w1_11")
         quantise_weight("w1_11")
-        load_weight("wb_0", wb[0:KP, :])
-        load_page(6)
-        load_weight("wb_1", wb[KP:H, :])
-        load_page(7)
         place_h1(2)
         read_page(2)
         deal_wa()
         place_h1(3)
         read_page(3)
+        xi0 = turned("wide", "xi0", [P, M, PACK], BF16, 1)
         nc.scalar.copy(xi0[:].rearrange("p (c i) t -> p c t i", i=4), xp0[:].rearrange("p t (c i) -> p c t i", i=4))
-        place_h1(4)
-        read_page(4)
-        place_h1(5)
         xq0 = held("xq0", [P, M], U32)
         xs0 = held("xs0", [P, M], U8)
         nc.vector.quantize_mx(out=xq0[:].bitcast(FP8X4), scales=xs0[:], in_=xi0[:].rearrange("p m t -> p (m t)"))
-        wb_grp = turned("planes", "wb_grp", [P, 2 * PACK * KP], BF16, 1)
-        place_h2(6)
-        round_weight("wb_0", wb_grp[:, : PACK * KP])
-        read_page(5)
+        tail = turned("wide", "tail", [P, M + S], F32, 1)
+        h1_last = make_h1(7, tail[:, M:])
+        for s in range(4, 6):
+            place_h1(s)
+            read_page(s)
         place_h1(6)
-        round_weight("wb_1", wb_grp[:, PACK * KP :])
-        quantise_weight("wb_0")
-        quantise_weight("wb_1")
-        tail = turned("planes", "tail", [P, M + 2 * S], F32, 1)
         read_page(6, tail[:, :M])
-        place_h1(7, tail[:, M : M + S])
-        place_h2(7, h2=tail[:, M + S :])
+        put_h1(7, h1_last)
 
         xq1 = []
         for c in range(M // XC):

from contextlib import ExitStack

import concourse.mybir as mybir

K, K2, T, T3, S, T2, H, N, M = 1024, 512, 2048, 1024, 512, 2048, 1024, 512, 1024
FLOPS = 2 * (K * H * S + K2 * H * S + 2 * H * N * M)

F32 = mybir.dt.float32
BF16 = mybir.dt.bfloat16
I32 = mybir.dt.int32
U32 = mybir.dt.uint32
U16 = mybir.dt.uint16
U8 = mybir.dt.uint8
FP8X4 = mybir.dt.float8_e4m3fn_x4
FP4X4 = mybir.dt.float4_e2m1fn_x4
ACT = mybir.ActivationFunctionType
MULT = mybir.AluOpType.mult
ADD = mybir.AluOpType.add

P = 128
PACK = 4
KP = P * PACK
XC = 256
YC = 128
ALIGN = 64


def tile_list_placement_office_slots_kernel(
    tc, tab_words, tab_scales, tab2_words, tab2_scales, offs, offs2, offs3, offs4, offs5,
    w1, w2_words, w2_scales, gain, wg1, wg2, page0, lean, wa_words, wa_scales, wb,
    out_0, out_1, out_2,
):
    nc = tc.nc
    with ExitStack() as ctx:
        keep = ctx.enter_context(tc.tile_pool(name="keep", bufs=1))
        ring = ctx.enter_context(tc.tile_pool(name="ring", bufs=2))
        psum = ctx.enter_context(tc.psum_pool(name="psum", bufs=8))

        def held(name, shape, dtype):
            return keep.tile(shape, dtype, name=name, align_bytes=ALIGN)

        def turned(tag, name, shape, dtype, bufs):
            return ring.tile(shape, dtype, name=name, tag=tag, bufs=bufs, align_bytes=ALIGN)

        def load_list(name, src):
            tile = held(name, [P, src.shape[1]], U16)
            nc.sync.dma_start(tile[:], src)
            return tile

        def words_of(src):
            return src.rearrange("p c i -> p (c i)").bitcast(I32)

        tab2s = held("tab2s", [P, T3], U8)
        nc.gpsimd.memset(tab2s[:].bitcast(I32), 0)
        w2s_raw = turned("yi", "w2s_raw", [P, KP], U8, 3)
        nc.gpsimd.memset(w2s_raw[:].bitcast(I32), 0)
        was_raw = turned("yi", "was_raw", [P, 2, N], U8, 3)
        nc.vector.memset(was_raw[:].bitcast(I32), 0)
        tabs = held("tabs", [P, T], U8)
        nc.vector.memset(tabs[:].bitcast(I32), 0)

        l2 = load_list("l2", offs2)
        tab2w = turned("tab2w", "tab2w", [P, T3], I32, 1)
        nc.sync.dma_start(tab2w[:], words_of(tab2_words[0]))
        for q in range(4):
            nc.sync.dma_start(tab2s[32 * q : 32 * q + 4, :].bitcast(I32), tab2_scales[0, 4 * q : 4 * q + 4, :].bitcast(I32))
        w2w_raw = turned("stage_c", "w2w_raw", [P, H], I32, 1)
        nc.sync.dma_start(w2w_raw[:], words_of(w2_words[0]))
        for q in range(4):
            nc.sync.dma_start(
                w2s_raw[32 * q : 32 * q + 8, :].bitcast(I32),
                w2_scales[0, 4 * q : 4 * q + 4, :].rearrange("r (b c) -> b r c", b=2).bitcast(I32),
            )
        gain_t = held("gain_t", [P, 2, PACK], F32)
        nc.sync.dma_start(gain_t[:], gain.rearrange("(b p t) -> p b t", b=2, t=PACK))

        def load_dealt(tag, name, src, first, last, upper_queue):
            tile = turned(tag, name, [P, last - first, S], F32, 1)
            for q in (0, 2, 1, 3):
                queue = nc.sync if q < 2 else upper_queue
                queue.dma_start(tile[32 * q : 32 * (q + 1)], src.rearrange("(q t) j -> q t j", t=PACK)[:, first:last, :])
            return [tile[:, t, :] for t in range(last - first)]

        page_rows = page0.rearrange("(b p t) c -> b t p c", b=2, t=PACK)
        pages = {}

        def load_page(s):
            pages[s] = held("page%d" % s, [P, T2], F32)
            nc.sync.dma_start(pages[s][:], page_rows[s // PACK, s % PACK])

        raws = {}

        def load_weight(name, src):
            raws[name] = turned("wraw", name + "_raw", [P, PACK, KP], F32, 3)
            nc.sync.dma_start(raws[name][:], src.rearrange("(p j) c -> p j c", j=PACK))

        load_page(0)
        l4 = load_list("l4", offs4)
        wg2d = load_dealt("wg2_first", "wg2_first", wg2, 0, 1, nc.sync)
        load_page(4)
        v2w = held("v2w", [P, S], U32)
        nc.vector.tensor_copy(v2w[:], tab2w[:].bitcast(U32).indirect(l2[:]))
        wg2d = wg2d + load_dealt("tab2w", "wg2_rest", wg2, 1, PACK, nc.gpsimd)
        load_page(1)
        l1 = load_list("l1", offs)
        tabw = []
        for a in range(2):
            tabw.append(turned("tabw%d" % a, "tabw%d" % a, [P, T], I32, 1))
            nc.sync.dma_start(tabw[a][:], words_of(tab_words[a]))
            for q in range(2 * a, 2 * a + 2):
                nc.sync.dma_start(tabs[32 * q : 32 * q + 8, :].bitcast(I32), tab_scales[:, 4 * q : 4 * q + 4, :].bitcast(I32))
        load_page(2)
        load_page(3)
        load_weight("w1_00", w1[0:KP, 0:KP])
        load_weight("w1_10", w1[KP:K, 0:KP])
        load_page(5)
        load_page(6)
        l3 = load_list("l3", offs3)

        v2s = held("v2s", [P, S], U8)
        nc.vector.tensor_copy(v2s[:], tab2s[:].indirect(l2[:]))
        w2w = held("w2w", [P, H], I32)
        nc.vector.tensor_copy(
            w2w[:].rearrange("p (b t q i) -> p b q t i", b=2, t=PACK, i=4), w2w_raw[:].rearrange("p (b q i t) -> p b q t i", b=2, t=PACK, i=4)
        )
        w2s = held("w2s", [P, KP], U8)
        nc.vector.tensor_copy(
            w2s[:].rearrange("p (t q i) -> p q t i", t=PACK, i=16), w2s_raw[:].rearrange("p (q i t) -> p q t i", t=PACK, i=16)
        )
        waw = held("waw", [P, 2, 2 * N], U8)
        was = held("was", [P, 2, N], U8)

        def deal_wa():
            nc.vector.tensor_copy(
                waw[:].bitcast(U16).rearrange("p a (t q i) -> p a q t i", t=PACK, i=8),
                waw_raw[:].bitcast(U16).rearrange("p a (q i t) -> p a q t i", t=PACK, i=8),
            )
            nc.vector.tensor_copy(
                was[:].rearrange("p a (t q i) -> p a q t i", t=PACK, i=16), was_raw[:].rearrange("p a (q i t) -> p a q t i", t=PACK, i=16)
            )

        def place_h2(s, first=0, last=S, h2=None):
            b, t = divmod(s, PACK)
            name = "%d_%d" % (s, first)
            bank = psum.tile([P, last - first], F32, name="h2ps" + name, tag="bank")
            nc.tensor.matmul_mx(
                out=bank[:], lhsT=w2w[:, s * P : (s + 1) * P].bitcast(FP8X4), lhsT_scale=w2s[4 * b : P, t * P : (t + 1) * P],
                rhs=v2w[:, first:last].bitcast(FP8X4), rhs_scale=v2s[:, first:last], start=True, stop=True,
            )
            if h2 is None:
                h2 = turned("h", "h2_" + name, [P, last - first], F32, 5)[:]
            nc.scalar.activation(h2, bank[:], ACT.Tanh)
            nc.scalar.activation(h2, h2, ACT.Copy, scale=gain_t[:, b, t : t + 1])
            nc.vector.tensor_tensor(pages[s][:].indirect(l4[:, first // 16 : last // 16]), h2, wg2d[t][:, first:last], MULT)

        codes = {}
        grouped = {}

        def round_weight(name, tile=None):
            grouped[name] = turned("stage_" + "ab"[int(name[3])], name + "_grp", [P, PACK * KP], BF16, 1)[:] if tile is None else tile
            nc.scalar.copy(
                grouped[name].rearrange("p (t m j) -> p m t j", t=PACK, j=PACK),
                raws[name][:].rearrange("p j (m t) -> p m t j", t=PACK),
            )

        def quantise_weight(name):
            words = held(name + "_w", [P, KP], U32)
            scales = held(name + "_s", [P, KP], U8)
            nc.vector.quantize_mx(out=words[:].bitcast(FP8X4), scales=scales[:], in_=grouped[name])
            codes[name] = (words, scales)

        place_h2(0, 0, S // 2)
        place_h2(0, S // 2, S)
        place_h2(4)
        place_h2(1)
        vw = []
        for a in range(2):
            vw.append(held("vw%d" % a, [P, S], U32))
            nc.vector.tensor_copy(vw[a][:], tabw[a][:].bitcast(U32).indirect(l1[:]))
        vs = held("vs", [P, S], U8)
        nc.vector.tensor_copy(vs[:], tabs[:].indirect(l1[:]))
        wg1d = load_dealt("tabw0", "wg1d", wg1, 0, PACK, nc.gpsimd)
        l5 = load_list("l5", offs5)
        load_page(7)
        lean_t = held("lean_t", [P, 2, PACK], F32)
        nc.sync.dma_start(lean_t[:], lean.rearrange("(b p t) -> p b t", b=2, t=PACK))
        load_weight("wb_0", wb[0:KP, :])
        load_weight("wb_1", wb[KP:H, :])
        load_weight("w1_01", w1[0:KP, KP:H])
        load_weight("w1_11", w1[KP:K, KP:H])
        waw_raw = turned("y", "waw_raw", [P, 2, 2 * N], U8, 4)
        nc.sync.dma_start(waw_raw[:].bitcast(I32), wa_words.rearrange("a p c -> p a c").bitcast(I32))
        for q in range(4):
            nc.sync.dma_start(
                was_raw[32 * q : 32 * q + 4].bitcast(I32),
                wa_scales[:, 4 * q : 4 * q + 4, :].rearrange("a r c -> r a c").bitcast(I32),
            )

        place_h2(2)
        place_h2(3)
        round_weight("w1_00")
        quantise_weight("w1_00")
        place_h2(5)
        round_weight("w1_10")
        quantise_weight("w1_10")
        place_h2(6)
        place_h2(7)

        def make_h1(s, h1=None):
            b, t = divmod(s, PACK)
            cols = slice(t * P, (t + 1) * P)
            bank = psum.tile([P, S], F32, name="h1ps%d" % s, tag="bank")
            for a in range(2):
                words, scales = codes["w1_%d%d" % (a, b)]
                nc.tensor.matmul_mx(
                    out=bank[:], lhsT=words[:, cols].bitcast(FP8X4), lhsT_scale=scales[:, cols],
                    rhs=vw[a][:].bitcast(FP8X4), rhs_scale=vs[4 * a : P, :], start=(a == 0), stop=(a == 1),
                )
            if h1 is None:
                h1 = turned("h", "h1_%d" % s, [P, S], F32, 5)[:]
            nc.scalar.activation(h1, bank[:], ACT.Abs)
            return h1

        def put_h1(s, h1):
            nc.vector.tensor_tensor(pages[s][:].indirect(l3[:]), h1, wg1d[s % PACK], MULT)

        def place_h1(s):
            put_h1(s, make_h1(s))

        xp0 = held("xp0", [P, PACK, M], BF16)
        xi1 = [held("xi1_%d" % c, [P, XC, PACK], BF16) for c in range(M // XC)]

        def shift(dst, src, s):
            b, t = divmod(s, PACK)
            nc.scalar.activation(dst, src, ACT.Identity, bias=lean_t[:, b, t : t + 1])

        def read_page(s, g=None):
            if g is None:
                g = turned("stage_" + "cababa"[s], "g%d" % s, [P, M], F32, 1)[:]
            nc.vector.tensor_copy(g, pages[s][:].indirect(l5[:]))
            if s < PACK:
                shift(xp0[:, s, :], g, s)
            else:
                for c in range(M // XC):
                    shift(xi1[c][:, :, s % PACK], g[:, c * XC : (c + 1) * XC], s)

        place_h1(0)
        read_page(0)
        wb_grp = turned("wide", "wb_grp", [P, 2 * PACK * KP], BF16, 1)
        round_weight("wb_0", wb_grp[:, : PACK * KP])
        round_weight("wb_1", wb_grp[:, PACK * KP :])
        quantise_weight("wb_0")
        quantise_weight("wb_1")
        round_weight("w1_01")
        quantise_weight("w1_01")
        place_h1(1)
        read_page(1)
        round_weight("w1_11")
        quantise_weight("w1_11")
        place_h1(2)
        read_page(2)
        deal_wa()
        place_h1(3)
        read_page(3)
        xi0 = turned("wide", "xi0", [P, M, PACK], BF16, 1)
        nc.scalar.copy(xi0[:].rearrange("p (c i) t -> p c t i", i=4), xp0[:].rearrange("p t (c i) -> p c t i", i=4))
        xq0 = held("xq0", [P, M], U32)
        xs0 = held("xs0", [P, M], U8)
        nc.vector.quantize_mx(out=xq0[:].bitcast(FP8X4), scales=xs0[:], in_=xi0[:].rearrange("p m t -> p (m t)"))
        tail = turned("wide", "tail", [P, M + S], F32, 1)
        h1_last = make_h1(7, tail[:, M:])
        for s in range(4, 6):
            place_h1(s)
            read_page(s)
        place_h1(6)
        read_page(6, tail[:, :M])
        put_h1(7, h1_last)

        xq1 = []
        for c in range(M // XC):
            g = held("glast%d" % c, [P, XC], F32)
            nc.vector.tensor_copy(g[:], pages[7][:].indirect(l5[:, c * XC // 16 : (c + 1) * XC // 16]))
            shift(xi1[c][:, :, PACK - 1], g[:], 7)
            words = held("xq1_%d" % c, [P, XC], U32)
            scales = held("xs1_%d" % c, [P, XC], U8)
            nc.vector.quantize_mx(out=words[:].bitcast(FP8X4), scales=scales[:], in_=xi1[c][:].rearrange("p m t -> p (m t)"))
            xq1.append((words, scales))

        yq = held("yq", [P, M], U32)
        ys = held("ys", [P, M], U8)
        y_rows = out_0.rearrange("(p t) m -> p t m", t=PACK)
        y_words = words_of(out_1[0])
        for c in range(M // YC):
            cols = slice(c * YC, (c + 1) * YC)
            ya = psum.tile([P, PACK, YC], F32, name="ya%d" % c, tag="bank")
            yb = psum.tile([P, PACK, YC], F32, name="yb%d" % c, tag="bank")
            for a in range(2):
                if a == 0:
                    x_words, x_scales = xq0[:, cols], xs0[:, cols]
                else:
                    part = slice(c * YC % XC, c * YC % XC + YC)
                    x_words, x_scales = xq1[c * YC // XC][0][:, part], xq1[c * YC // XC][1][:, part]
                b_words, b_scales = codes["wb_%d" % a]
                for t in range(PACK):
                    nc.tensor.matmul_mx(
                        out=yb[:, t, :], lhsT=b_words[:, t * P : (t + 1) * P].bitcast(FP8X4), lhsT_scale=b_scales[:, t * P : (t + 1) * P],
                        rhs=x_words.bitcast(FP8X4), rhs_scale=x_scales, start=(a == 0 and t == 0), stop=(a == 1 and t == PACK - 1),
                    )
                for t in range(PACK):
                    nc.tensor.matmul_mx(
                        out=ya[:, t, :], lhsT=waw[:, a, 2 * t * P : 2 * (t + 1) * P].bitcast(FP4X4), lhsT_scale=was[:, a, t * P : (t + 1) * P],
                        rhs=x_words.bitcast(FP8X4), rhs_scale=x_scales, start=(a == 0 and t == 0), stop=(a == 1 and t == PACK - 1),
                    )
            yb_sb = turned("h", "yb_sb%d" % c, [P, PACK, YC], F32, 5)
            nc.scalar.copy(yb_sb[:], yb[:])
            y = turned("y", "y%d" % c, [P, PACK, YC], F32, 4)
            nc.vector.scalar_tensor_tensor(y[:], yb_sb[:], 1.0, ya[:], ADD, MULT)
            nc.vector.tensor_tensor(y[:], y[:], yb_sb[:], ADD)
            nc.sync.dma_start(y_rows[:, :, cols], y[:])
            yi = turned("yi", "yi%d" % c, [P, YC, PACK], BF16, 3)
            nc.scalar.copy(
                yi[:].rearrange("p (c i) t -> p c t i", i=4), y[:].rearrange("p t (c i) -> p c t i", i=4)
            )
            nc.vector.quantize_mx(out=yq[:, cols].bitcast(FP8X4), scales=ys[:, cols], in_=yi[:].rearrange("p m t -> p (m t)"))
            if c % 2 == 1:
                pair = slice((c - 1) * YC, (c + 1) * YC)
                nc.sync.dma_start(y_words[:, pair], yq[:, pair].bitcast(I32))
        for q in range(4):
            nc.scalar.dma_start(out_2[0, 4 * q : 4 * q + 4, :].bitcast(I32), ys[32 * q : 32 * q + 4, :].bitcast(I32))
